import numpy as np
import ml_dtypes


def mxq(x, axis, fmt="e4m3"):
    dtype, down = {"e4m3": (ml_dtypes.float8_e4m3fn, 7), "e5m2": (ml_dtypes.float8_e5m2, 14)}[fmt]
    v = np.moveaxis(np.asarray(x, np.float32).astype(ml_dtypes.bfloat16).astype(np.float64), axis, -1)
    blocks = v.reshape(v.shape[:-1] + (-1, 32))
    amax = np.abs(blocks).max(-1, keepdims=True)
    byte = np.maximum(np.where(amax > 0, np.frexp(amax)[1] - 1 + 127, 0) - down, 1)
    scale = np.exp2(byte - 127.0)
    codes = (blocks / scale).astype(np.float32).astype(dtype).astype(np.float64)
    return np.moveaxis((codes * scale).reshape(v.shape), -1, axis)


WIDE = False


def mx_kscale(k):
    if not WIDE:
        return np.ones(k)
    levels = np.array([10, -10, 5, -5, 0])
    if k % 512:
        return np.exp2(np.random.permutation(np.resize(levels, k // 32))).repeat(32)
    a = np.empty((k // 512, 16))
    for p in range(k // 512):
        a[p, :8] = np.random.permutation(np.resize(levels, 8))
        for g in range(8):
            far = levels[np.abs(levels - a[p, g]) >= 10]
            a[p, g + 8] = far[np.random.randint(len(far))]
    return np.exp2(a.ravel()).repeat(32)


BF16 = ml_dtypes.bfloat16


def bf(x):
    return np.asarray(x, np.float32).astype(BF16)


def f64(x):
    return np.asarray(x).astype(np.float64)


E2M1 = np.array([0.0, 0.5, 1.0, 1.5, 2.0, 3.0, 4.0, 6.0, -0.0, -0.5, -1.0, -1.5, -2.0, -3.0, -4.0, -6.0])


def pack_weight(w, fmt):
    k, n = w.shape
    w = f64(bf(w)).reshape(k // 32, 32, n)
    amax = np.abs(w).max(1)
    if fmt == "e4m3":
        byte = np.frexp(amax)[1] - 1 + 127 - 7
    else:
        mant, ex = np.frexp(amax / 6.0)
        byte = np.where(mant > 0.5, ex, ex - 1) + 127
    byte = np.clip(np.where(amax > 0, byte, 1), 1, 254)
    scaled = (w * np.exp2(127.0 - byte)[:, None, :]).reshape(k, n).astype(np.float32)
    by_word = np.ascontiguousarray(scaled.reshape(k // 512, 128, 4, n).transpose(0, 1, 3, 2))
    if fmt == "e4m3":
        words = by_word.astype(ml_dtypes.float8_e4m3fn).view(np.uint8)
    else:
        c = by_word.astype(ml_dtypes.float4_e2m1fn).view(np.uint8) & 0xF
        words = c[..., 0::2] | (c[..., 1::2] << 4)
    return np.ascontiguousarray(words), np.ascontiguousarray(byte.astype(np.uint8).reshape(k // 512, 16, n))


def unpack_weight(words, scales, fmt):
    g, p, n, _ = words.shape
    if fmt == "e4m3":
        vals = np.ascontiguousarray(words).view(ml_dtypes.float8_e4m3fn).astype(np.float64)
    else:
        nib = np.empty((g, p, n, 4), np.uint8)
        nib[..., 0::2] = words & 0xF
        nib[..., 1::2] = words >> 4
        vals = E2M1[nib]
    vals = vals * np.repeat(np.exp2(scales.astype(np.float64) - 127.0), 8, axis=1)[..., None]
    return vals.transpose(0, 1, 3, 2).reshape(g * 512, n)
def pack4(w):
    words, scales = pack_weight(w, "e2m1")
    return words.reshape(words.shape[0], 128, -1), scales


def unpack4(words, scales):
    return unpack_weight(words.reshape(words.shape[0], 128, -1, 2), scales, "e2m1")


E4M3FN = np.array([(-1.0 if i & 128 else 1.0) * ((1.0 + (i & 7) / 8.0) * 2.0 ** (((i >> 3) & 15) - 7) if i & 120 else (i & 7) * 2.0 ** -9) for i in range(256)])


def e4m3fn_bytes(y):
    return np.clip(np.asarray(y, np.float64), -448.0, 448.0).astype(np.float32).astype(ml_dtypes.float8_e4m3fn).view(np.uint8)


def e4m3fn_values(b):
    return E4M3FN[b]


L, D, F, P = 128, 1024, 512, 128
F2 = 2 * F


def draw0():
    u = mx_kscale(D)
    t = mx_kscale(F2)
    s = bf(np.random.standard_normal((L, D)) * u)
    w1_words, w1_scales = pack4(np.random.standard_normal((D, F2)) / np.sqrt(D) / u[:, None])
    b1 = bf(np.random.standard_normal(F2) * 0.3)
    g = bf((1.0 + 0.1 * np.random.standard_normal(F2)) * t)
    wo_words, wo_scales = pack4(np.random.standard_normal((F2, P)) / np.sqrt(F2) / t[:, None])
    bo = bf(np.random.standard_normal(P) * 0.3)
    return {
        "s": s,
        "w1_words": w1_words,
        "w1_scales": w1_scales,
        "b1": b1,
        "g": g,
        "wo_words": wo_words,
        "wo_scales": wo_scales,
        "bo": bo,
    }


def core(s, w1_words, w1_scales, b1, g, wo_words, wo_scales, bo):
    h = (mxq(f64(s), 1, "e4m3") @ unpack4(w1_words, w1_scales)) + f64(b1)
    q = h[:, 0:F]
    k = h[:, F:F2]
    q_j = q[None, :, :]
    k_i = k[:, None, :]
    prod = q_j * k_i
    diff = q_j - k_i
    c = np.concatenate([prod, diff], axis=-1) * f64(g)
    return (mxq(c, 2, "e4m3") @ unpack4(wo_words, wo_scales)) + f64(bo)


def setup_inputs():
    drawn = draw0()
    full = np.asarray(drawn['s']).astype(np.float64)
    scale = (np.abs(full).reshape(128, 8, 128).max(axis=(2,)) / 448.0).astype(np.float32)
    given = {}
    for key, value in drawn.items():
        if key == 's':
            given['s_bytes'] = e4m3fn_bytes(full / np.repeat(scale.astype(np.float64), 128, axis=1))
            given['s_scale'] = scale
        else:
            given[key] = value
    return given


def reference(s_bytes, s_scale, w1_words, w1_scales, b1, g, wo_words, wo_scales, bo):
    return core(e4m3fn_values(s_bytes) * np.repeat(s_scale.astype(np.float64), 128, axis=1), w1_words, w1_scales, b1, g, wo_words, wo_scales, bo)

@@ -1,0 +1,426 @@
+from contextlib import ExitStack
+
+import concourse.mybir as mybir
+from concourse.masks import make_identity
+
+L, D, F, C = 128, 1024, 512, 128
+FLOPS = 2 * L * D * 2 * F + 2 * L * L * 2 * F * C
+
+F32 = mybir.dt.float32
+BF16 = mybir.dt.bfloat16
+I32 = mybir.dt.int32
+U32 = mybir.dt.uint32
+U8 = mybir.dt.uint8
+FP8 = mybir.dt.float8_e4m3fn
+FP8X4 = mybir.dt.float8_e4m3fn_x4
+FP4X4 = mybir.dt.float4_e2m1fn_x4
+ALU = mybir.AluOpType
+ACT = mybir.ActivationFunctionType
+
+P = 128
+PACK = 4
+CLASSES = 4
+SPAN = L // CLASSES
+RUN = 6
+BLOCKS = 4
+PARK = 124
+GPSIMD_ROWS = 13
+
+
+def plan():
+    groups = [
+        dict_group(None, None, [24, 25, 26, 27], 0, 2, 14),
+        dict_group(None, None, list(range(56, 64)), 0, 3, 16),
+    ]
+    singles = [28, 29, 30, 31] + list(range(88, 96)) + [120, 121, 122, 123]
+    for m in range(BLOCKS * CLASSES):
+        groups.append(dict_group(m // CLASSES, m % CLASSES, [singles[m]], 0 if m % 3 == 0 else 1, 0, GPSIMD_ROWS))
+    groups.append(dict_group(None, None, [124, 125, 126, 127], 0, 0, 12))
+    return groups
+
+
+def dict_group(block, turn, fixed, s_prods, v_diffs, g_rows):
+    shifted = 0 if block is None else RUN
+    units = shifted + len(fixed)
+    on_scalar = [("diff", u) for u in range(units - v_diffs)] + [("prod", u) for u in range(units - s_prods, units)]
+    on_vector = [("prod", u) for u in range(units - s_prods)] + [("diff", u) for u in range(units - v_diffs, units)]
+    return {
+        "block": block, "turn": turn, "fixed": fixed, "shifted": shifted, "units": units,
+        "s_prods": s_prods, "v_diffs": v_diffs, "g_rows": g_rows, "on_scalar": on_scalar, "on_vector": on_vector,
+    }
+
+
+def power_of_two_runs(count):
+    runs, start = [], 0
+    for width in (8, 4, 2, 1):
+        while count - start >= width:
+            runs.append((start, width))
+            start += width
+    return runs
+
+
+def tile_esmfoldsequencetopairproductdifference_d1p_kernel(
+    tc, s_bytes, s_scale, w1_words, w1_scales, b1, g, wo_words, wo_scales, bo, out
+):
+    nc = tc.nc
+    groups = plan()
+
+    with ExitStack() as ctx:
+        keep = ctx.enter_context(tc.tile_pool(name="keep", bufs=1))
+        work = ctx.enter_context(tc.tile_pool(name="work", bufs=2))
+        psum = ctx.enter_context(tc.psum_pool(name="psum", bufs=1))
+        ctx.enter_context(tc.manual_schedule())
+
+        def bank(index, name):
+            return psum.tile([P, 512], F32, name=name, tag="bank%d" % index)
+
+        s_u8 = keep.tile([P, D], U8, name="s_u8")
+        s_sc = keep.tile([P, D // P], F32, name="s_sc")
+        w1_w = keep.tile([P, 2, 2 * D], U8, name="w1_w", align_bytes=64)
+        w1_s = keep.tile([P, 2, D], U8, name="w1_s", align_bytes=64)
+        wo_w = keep.tile([P, 2, 2 * C], U8, name="wo_w", align_bytes=64)
+        wo_s = keep.tile([P, 2, C], U8, name="wo_s", align_bytes=64)
+        rows = keep.tile([P, 2 * D + C], BF16, name="rows")
+        g2_cols = keep.tile([P, PACK], BF16, name="g2_cols")
+        neg_g2 = keep.tile([P, PACK], F32, name="neg_g2")
+        ones = keep.tile([P, P], BF16, name="ones")
+        perm = keep.tile([P, CLASSES, P], F32, name="perm")
+        warm = keep.tile([P, 1], F32, name="warm")
+
+        nc.vector.memset(w1_s[:].rearrange("p g n -> p (g n)").bitcast(I32), 0)
+        nc.vector.memset(rows[:].bitcast(I32), 0)
+        nc.vector.memset(wo_s[:].rearrange("p g n -> p (g n)").bitcast(I32), 0)
+        make_identity(nc, perm[:, 0, :])
+        nc.gpsimd.memset(ones[:], 1.0)
+        ident = perm[:, 0, :]
+        nc.scalar.activation(out=warm[:], in_=perm[:, 0, 0:1], func=ACT.Identity)
+
+        nc.sync.dma_start(out=s_u8[:], in_=s_bytes)
+        nc.sync.dma_start(out=s_sc[:], in_=s_scale)
+        for quad in range(4):
+            nc.sync.dma_start(
+                out=w1_s[32 * quad : 32 * quad + 4, :, :].bitcast(I32),
+                in_=w1_scales[:, 4 * quad : 4 * quad + 4, :].rearrange("g q n -> q g n").bitcast(I32),
+            )
+        nc.sync.dma_start(out=rows[0:1, 0:D], in_=b1.rearrange("(o n) -> o n", o=1))
+        for half in range(2):
+            nc.sync.dma_start(out=w1_w[:, half, :].bitcast(I32), in_=w1_words[half].bitcast(I32))
+        nc.sync.dma_start(out=rows[0:1, D : 2 * D], in_=g.rearrange("(o n) -> o n", o=1))
+        nc.sync.dma_start(out=rows[0:1, 2 * D : 2 * D + C], in_=bo.rearrange("(o n) -> o n", o=1))
+        nc.sync.dma_start(out=g2_cols[:], in_=g[F : 2 * F].rearrange("(p t) -> p t", t=PACK))
+        for quad in range(4):
+            nc.sync.dma_start(
+                out=wo_s[32 * quad : 32 * quad + 4, :, :].bitcast(I32),
+                in_=wo_scales[:, 4 * quad : 4 * quad + 4, :].rearrange("g q n -> q g n").bitcast(I32),
+            )
+        nc.sync.dma_start(out=wo_w[:].bitcast(I32), in_=wo_words.rearrange("g p n -> p g n").bitcast(I32))
+
+        s_bf = keep.tile([P, D], BF16, name="s_bf")
+        for blk in range(D // P):
+            cols = slice(blk * P, (blk + 1) * P)
+            if blk < 5:
+                nc.vector.tensor_scalar(
+                    out=s_bf[:, cols], in0=s_u8[:, cols].bitcast(FP8), scalar1=s_sc[:, blk : blk + 1], scalar2=None, op0=ALU.mult
+                )
+            else:
+                nc.scalar.activation(out=s_bf[:, cols], in_=s_u8[:, cols].bitcast(FP8), func=ACT.Copy, scale=s_sc[:, blk : blk + 1])
+        s_words = s_bf[:].bitcast(F32)
+        s_turned = bank(3, "s_turned")
+        for half in range(2):
+            for u in range(2):
+                at = (2 * half + u) * P
+                nc.tensor.transpose(s_turned[:, at : at + P], s_words[:, 256 * half + u : 256 * (half + 1) : 2], ident)
+        s_grp = keep.tile([P, 2 * L * PACK], BF16, name="s_grp", align_bytes=64)
+        nc.vector.tensor_copy(
+            out=s_grp[:].bitcast(F32).rearrange("p (g r u) -> p g r u", g=2, u=2),
+            in_=s_turned[:].rearrange("p (g u r) -> p g r u", g=2, u=2),
+        )
+        nc.vector.tensor_scalar(out=neg_g2[:], in0=g2_cols[:], scalar1=-1.0, scalar2=None, op0=ALU.mult)
+        s_codes = keep.tile([P, 2 * L], U32, name="s_codes", align_bytes=64)
+        s_scales = keep.tile([P, 2 * L], U8, name="s_scales", align_bytes=64)
+        nc.vector.quantize_mx(out=s_codes[:].bitcast(FP8X4), scales=s_scales[:], in_=s_grp[:])
+
+        for turn in range(1, CLASSES):
+            dst = perm[:, turn, :].rearrange("p (b a) -> p b a", a=CLASSES)
+            src = ident.rearrange("p (b a) -> p b a", a=CLASSES)
+            nc.scalar.copy(out=dst[:, :, 0 : CLASSES - turn], in_=src[:, :, turn:CLASSES])
+            nc.scalar.copy(out=dst[:, :, CLASSES - turn : CLASSES], in_=src[:, :, 0:turn])
+
+        def spread(index, name, first):
+            spread_bank = bank(index, name)
+            nc.tensor.matmul(
+                out=spread_bank[:].rearrange("m (t p) -> m t p", t=PACK),
+                lhsT=ones[:],
+                rhs=rows[:, first : first + F].rearrange("k (p t) -> k t p", t=PACK),
+                start=True,
+                stop=True,
+            )
+            return spread_bank
+
+        b1_sb = keep.tile([P, 2, F], F32, name="b1_sb")
+        for half in range(2):
+            b1_bank = spread(4 + half, "b1_bank%d" % half, half * F)
+            nc.scalar.copy(out=b1_sb[:, half, :], in_=b1_bank[:])
+
+        h_banks = []
+        for half in range(2):
+            h_bank = bank(1 + half, "h_bank%d" % half)
+            for ps in range(2):
+                nc.tensor.matmul_mx(
+                    out=h_bank[:],
+                    lhsT=s_codes[:, ps * L : (ps + 1) * L].bitcast(FP8X4),
+                    lhsT_scale=s_scales[:, ps * L : (ps + 1) * L],
+                    rhs=w1_w[:, ps, half * 2 * F : (half + 1) * 2 * F].bitcast(FP4X4),
+                    rhs_scale=w1_s[:, ps, half * F : (half + 1) * F],
+                    start=(ps == 0),
+                    stop=(ps == 1),
+                )
+            h_banks.append(h_bank)
+        g1_bank = spread(6, "g1_bank", D)
+        g2_bank = spread(7, "g2_bank", D + F)
+        bo_bank = bank(0, "bo_bank")
+        nc.tensor.matmul(out=bo_bank[:, 0:C], lhsT=ones[:], rhs=rows[:, 2 * D : 2 * D + C], start=True, stop=True)
+        bo_sb = keep.tile([P, C], F32, name="bo_sb")
+        nc.scalar.copy(out=bo_sb[:], in_=bo_bank[:, 0:C])
+
+        q_tok = keep.tile([P, F], F32, name="q_tok")
+        k_tok = keep.tile([P, F], F32, name="k_tok")
+        qg1_tok = keep.tile([P, F], F32, name="qg1_tok")
+        qg2_tok = keep.tile([P, F], F32, name="qg2_tok")
+        nkg2_tok = keep.tile([P, F], F32, name="nkg2_tok")
+        for half, dst in enumerate((q_tok, k_tok)):
+            nc.vector.tensor_tensor(
+                out=dst[:].rearrange("i (t p) -> i t p", t=PACK),
+                in0=h_banks[half][:].rearrange("i (p t) -> i t p", t=PACK),
+                in1=b1_sb[:, half, :].rearrange("i (t p) -> i t p", t=PACK),
+                op=ALU.add,
+            )
+        nc.vector.tensor_tensor(out=qg1_tok[:], in0=q_tok[:], in1=g1_bank[:], op=ALU.mult)
+        nc.vector.tensor_tensor(out=qg2_tok[:], in0=q_tok[:], in1=g2_bank[:], op=ALU.mult)
+        nc.vector.scalar_tensor_tensor(out=nkg2_tok[:], in0=k_tok[:], scalar=-1.0, in1=g2_bank[:], op0=ALU.mult, op1=ALU.mult)
+        parked = out[:, PARK : PARK + PACK, :].rearrange("i j c -> i (j c)")
+        nc.sync.dma_start(out=parked, in_=qg2_tok[:])
+
+        def turn_tokens(index, name, src, interleave):
+            turned = bank(index, name)
+            for t in range(PACK):
+                if interleave:
+                    dst = turned[:].rearrange("p (n t) -> p n t", t=PACK)[:, :, t]
+                else:
+                    dst = turned[:, t * P : (t + 1) * P]
+                nc.tensor.transpose(dst, src[:, t * P : (t + 1) * P], ident)
+            return turned
+
+        k_bank = turn_tokens(0, "k_bank", k_tok, True)
+        qg1_bank = turn_tokens(3, "qg1_bank", qg1_tok, False)
+        qg2_bank = turn_tokens(4, "qg2_bank", qg2_tok, False)
+        nkg2_bank = turn_tokens(5, "nkg2_bank", nkg2_tok, True)
+
+        k_sb = keep.tile([P, F], F32, name="k_sb")
+        k_planes = keep.tile([P, PACK, L], F32, name="k_planes")
+        qg1 = keep.tile([P, SPAN, 2 * CLASSES * PACK], F32, name="qg1")
+        qg2 = keep.tile([P, L, PACK], F32, name="qg2")
+        nc.scalar.copy(out=k_sb[:], in_=k_bank[:])
+        nc.scalar.copy(out=k_planes[:], in_=k_bank[:].rearrange("p (n t) -> p t n", t=PACK))
+        nc.vector.tensor_copy(
+            out=qg1[:, :, 0:16].rearrange("p r (a t) -> p r a t", t=PACK),
+            in_=qg1_bank[:].rearrange("p (t a r) -> p r a t", t=PACK, a=CLASSES),
+        )
+        nc.scalar.copy(out=qg2[:], in_=qg2_bank[:].rearrange("p (t j) -> p j t", t=PACK))
+        nc.scalar.copy(out=qg1[:, :, 16:28], in_=qg1[:, :, 0:12])
+
+        q_rep = [keep.tile([P, RUN, F], F32, name="q_rep%d" % block) for block in range(BLOCKS)]
+
+        def load_replicas(block):
+            for a in range(CLASSES):
+                first = SPAN * a + RUN * block
+                nc.sync.dma_start(
+                    out=q_rep[block][a:P:CLASSES, :, :], in_=parked[first : first + RUN, :].partition_broadcast(SPAN)
+                )
+
+        c_scalar, c_vector, codes, results = {}, {}, {}, {}
+        diff_banks = [3, 4, 6, 7, 5]
+        diff_count = [0]
+
+        def fixed_on_scalar(kind, j, dst):
+            planes = work.tile([P, PACK, L], BF16, name="planes", tag="planes", bufs=3)
+            for t in range(PACK):
+                if kind == "diff":
+                    nc.scalar.activation(
+                        out=planes[:, t, :], in_=k_planes[:, t, :], func=ACT.Identity,
+                        scale=neg_g2[:, t : t + 1], bias=qg2[:, j, t : t + 1],
+                    )
+                else:
+                    at = PACK * (j // SPAN) + t
+                    nc.scalar.activation(
+                        out=planes[:, t, :], in_=k_planes[:, t, :], func=ACT.Copy, scale=qg1[:, j % SPAN, at : at + 1]
+                    )
+
+            def interleave():
+                nc.scalar.copy(
+                    out=dst.rearrange("p (c i t) -> p c t i", i=4, t=PACK),
+                    in_=planes[:].rearrange("p t (c i) -> p c t i", i=4),
+                )
+
+            return interleave
+
+        def shifted_diff(grp, u, dst):
+            index = diff_banks[diff_count[0] % len(diff_banks)]
+            diff_count[0] += 1
+            diff_bank = bank(index, "diff_bank")
+            for t in range(PACK):
+                cols = slice(t * P, (t + 1) * P)
+                nc.tensor.matmul(
+                    out=diff_bank[:, cols], lhsT=nkg2_tok[:, cols], rhs=ident, is_transpose=True, start=True, stop=False
+                )
+                nc.tensor.matmul(
+                    out=diff_bank[:, cols], lhsT=q_rep[grp["block"]][:, u, cols], rhs=perm[:, grp["turn"], :],
+                    is_transpose=True, start=False, stop=True,
+                )
+            nc.scalar.copy(
+                out=dst.rearrange("p (n t) -> p n t", t=PACK), in_=diff_bank[:].rearrange("p (t n) -> p n t", t=PACK)
+            )
+
+        def scalar_work(m):
+            grp = groups[m]
+            tile = work.tile([P, 8, F], BF16, name="c_scalar", tag="c_scalar", align_bytes=64)
+            c_scalar[m] = tile
+            slots = list(enumerate(grp["on_scalar"]))
+            ahead = min(2, grp["shifted"])
+            slots = slots[:ahead] + slots[grp["shifted"] :] + slots[ahead : grp["shifted"]]
+            pending = None
+            for slot, (kind, u) in slots:
+                following = None
+                if u < grp["shifted"]:
+                    shifted_diff(grp, u, tile[:, slot, :])
+                else:
+                    following = fixed_on_scalar(kind, grp["fixed"][u - grp["shifted"]], tile[:, slot, :])
+                if pending is not None:
+                    pending()
+                pending = following
+            if pending is not None:
+                pending()
+
+        def products(engine, k_src, grp, tile, first, count, row0, row1):
+            lo, hi = 16 * row0, 16 * row1
+            if first < grp["shifted"]:
+                inner = 16
+                tau = RUN * grp["block"] + first
+                at = PACK * grp["turn"]
+            else:
+                inner = PACK
+                j = grp["fixed"][first - grp["shifted"]]
+                tau = j % SPAN
+                at = PACK * (j // SPAN)
+            shape = [P, count, (hi - lo) // inner, inner]
+            engine.tensor_tensor(
+                out=tile[:, first : first + count, lo:hi].rearrange("p u (b x) -> p u b x", x=inner),
+                in0=k_src[:, lo:hi].rearrange("p (b x) -> p b x", x=inner).unsqueeze(1).to_broadcast(shape),
+                in1=qg1[:, tau : tau + count, at : at + inner].unsqueeze(2).to_broadcast(shape),
+                op=ALU.mult,
+            )
+
+        def evacuate(m, half):
+            grp = groups[m]
+            count = min(4, grp["units"] - 4 * half)
+            if count <= 0:
+                return
+            acc, result = results[m]
+            nc.vector.tensor_tensor(
+                out=result[:, 4 * half : 4 * half + count, :],
+                in0=acc[half][:, 0 : count * C].rearrange("p (u c) -> p u c", c=C),
+                in1=bo_sb[:].unsqueeze(1).to_broadcast([P, count, C]),
+                op=ALU.add,
+            )
+
+        def store(m):
+            grp = groups[m]
+            result = results[m][1]
+            shifted = grp["shifted"]
+            if shifted:
+                for a in range(CLASSES):
+                    j = SPAN * ((a + grp["turn"]) % CLASSES) + RUN * grp["block"]
+                    nc.sync.dma_start(out=out[a:L:CLASSES, j : j + RUN, :], in_=result[a:P:CLASSES, 0:RUN, :])
+            j = grp["fixed"][0]
+            count = len(grp["fixed"])
+            nc.sync.dma_start(out=out[:, j : j + count, :], in_=result[:, shifted : shifted + count, :])
+
+        def vector_work(m):
+            grp = groups[m]
+            tile = work.tile([P, 11, F], BF16, name="c_vector", tag="c_vector", bufs=1, align_bytes=64)
+            c_vector[m] = tile
+            shared = grp["shifted"] if grp["shifted"] else grp["units"]
+            split = SPAN - grp["g_rows"]
+            products(nc.gpsimd, k_sb, grp, tile, 0, shared, split, SPAN)
+            products(nc.vector, k_bank, grp, tile, 0, shared // 2, 0, split)
+            if m:
+                evacuate(m - 1, 0)
+            products(nc.vector, k_bank, grp, tile, shared // 2, shared // 2, 0, split)
+            if m:
+                evacuate(m - 1, 1)
+                store(m - 1)
+            if grp["shifted"] and not grp["s_prods"]:
+                products(nc.vector, k_bank, grp, tile, shared, 1, 0, SPAN)
+            if grp["v_diffs"]:
+                count = grp["v_diffs"]
+                j = grp["fixed"][grp["units"] - count]
+                shape = [P, count, L, PACK]
+                nc.vector.tensor_tensor(
+                    out=tile[:, grp["units"] : grp["units"] + count, :].rearrange("p u (n t) -> p u n t", t=PACK),
+                    in0=nkg2_bank[:].rearrange("p (n t) -> p n t", t=PACK).unsqueeze(1).to_broadcast(shape),
+                    in1=qg2[:, j : j + count, :].unsqueeze(2).to_broadcast(shape),
+                    op=ALU.add,
+                )
+
+        def quantise(m):
+            grp = groups[m]
+            where = {}
+            for name, tile, halves, most in (
+                ("s", c_scalar[m], grp["on_scalar"], 8), ("v", c_vector[m], grp["on_vector"], 11)
+            ):
+                words = work.tile([P, most * L], U32, name="words_" + name, tag="words_" + name, align_bytes=64)
+                scales = work.tile([P, most * L], U8, name="scales_" + name, tag="scales_" + name, align_bytes=64)
+                for start, width in power_of_two_runs(len(halves)):
+                    cols = slice(start * L, (start + width) * L)
+                    nc.vector.quantize_mx(
+                        out=words[:, cols].bitcast(FP8X4),
+                        scales=scales[:, cols],
+                        in_=tile[:, start : start + width, :].rearrange("p u x -> p (u x)"),
+                    )
+                for slot, half in enumerate(halves):
+                    cols = slice(slot * L, (slot + 1) * L)
+                    where[half] = (words[:, cols], scales[:, cols])
+            codes[m] = where
+
+        def multiply(m):
+            grp = groups[m]
+            acc = [bank(1 + half, "acc%d" % half) for half in range((grp["units"] + 3) // 4)]
+            for u in range(grp["units"]):
+                for ps, kind in enumerate(("prod", "diff")):
+                    words, scales = codes[m][(kind, u)]
+                    nc.tensor.matmul_mx(
+                        out=acc[u // 4][:, (u % 4) * C : (u % 4 + 1) * C],
+                        lhsT=words.bitcast(FP8X4),
+                        lhsT_scale=scales,
+                        rhs=wo_w[:, ps, :].bitcast(FP4X4),
+                        rhs_scale=wo_s[:, ps, :],
+                        start=(ps == 0),
+                        stop=(ps == 1),
+                    )
+            result = work.tile([P, 8, C], F32, name="result", tag="result", bufs=3)
+            results[m] = (acc, result)
+
+        load_replicas(0)
+        scalar_work(0)
+        for m in range(len(groups)):
+            vector_work(m)
+            if 1 <= m < BLOCKS:
+                load_replicas(m)
+            if m + 1 < len(groups):
+                scalar_work(m + 1)
+            quantise(m)
+            multiply(m)
+        last = len(groups) - 1
+        evacuate(last, 0)
+        evacuate(last, 1)
+        store(last)

@@ -24,7 +24,7 @@ SPAN = L // CLASSES
 RUN = 6
 BLOCKS = 4
 PARK = 124
-GPSIMD_ROWS = 13
+GPSIMD_ROWS = 12
 
 
 def plan():
@@ -34,7 +34,7 @@ def plan():
     ]
     singles = [28, 29, 30, 31] + list(range(88, 96)) + [120, 121, 122, 123]
     for m in range(BLOCKS * CLASSES):
-        groups.append(dict_group(m // CLASSES, m % CLASSES, [singles[m]], 0 if m % 3 == 0 else 1, 0, GPSIMD_ROWS))
+        groups.append(dict_group(m // CLASSES, m % CLASSES, [singles[m]], 1 if m % 3 == 2 else 0, 0, GPSIMD_ROWS))
     groups.append(dict_group(None, None, [124, 125, 126, 127], 0, 0, 12))
     return groups
 
@@ -80,71 +80,40 @@ def tile_esmfoldsequencetopairproductdifference_d1p_kernel(
         w1_s = keep.tile([P, 2, D], U8, name="w1_s", align_bytes=64)
         wo_w = keep.tile([P, 2, 2 * C], U8, name="wo_w", align_bytes=64)
         wo_s = keep.tile([P, 2, C], U8, name="wo_s", align_bytes=64)
-        rows = keep.tile([P, 2 * D + C], BF16, name="rows")
-        g2_cols = keep.tile([P, PACK], BF16, name="g2_cols")
+        rows = keep.tile([P, D + F + C], BF16, name="rows")
+        g_cols = keep.tile([P, 2, PACK], BF16, name="g_cols")
         neg_g2 = keep.tile([P, PACK], F32, name="neg_g2")
         ones = keep.tile([P, P], BF16, name="ones")
         perm = keep.tile([P, CLASSES, P], F32, name="perm")
         warm = keep.tile([P, 1], F32, name="warm")
 
-        nc.vector.memset(w1_s[:].rearrange("p g n -> p (g n)").bitcast(I32), 0)
         nc.vector.memset(rows[:].bitcast(I32), 0)
+        nc.vector.memset(w1_s[:].rearrange("p g n -> p (g n)").bitcast(I32), 0)
         nc.vector.memset(wo_s[:].rearrange("p g n -> p (g n)").bitcast(I32), 0)
-        make_identity(nc, perm[:, 0, :])
         nc.gpsimd.memset(ones[:], 1.0)
+        make_identity(nc, perm[:, 0, :])
         ident = perm[:, 0, :]
-        nc.scalar.activation(out=warm[:], in_=perm[:, 0, 0:1], func=ACT.Identity)
+        nc.scalar.activation(out=warm[:], in_=ones[:, 0:1], func=ACT.Identity)
 
         nc.sync.dma_start(out=s_u8[:], in_=s_bytes)
         nc.sync.dma_start(out=s_sc[:], in_=s_scale)
+        nc.sync.dma_start(out=rows[0:1, 0:D], in_=b1.rearrange("(o n) -> o n", o=1))
+        nc.sync.dma_start(out=rows[0:1, D : D + F], in_=g[F : 2 * F].rearrange("(o n) -> o n", o=1))
+        nc.sync.dma_start(out=rows[0:1, D + F : D + F + C], in_=bo.rearrange("(o n) -> o n", o=1))
+        for half in range(2):
+            nc.sync.dma_start(out=w1_w[:, half, :].bitcast(I32), in_=w1_words[half].bitcast(I32))
+        nc.sync.dma_start(out=g_cols[:], in_=g.rearrange("(h p t) -> p h t", h=2, t=PACK))
         for quad in range(4):
             nc.sync.dma_start(
                 out=w1_s[32 * quad : 32 * quad + 4, :, :].bitcast(I32),
                 in_=w1_scales[:, 4 * quad : 4 * quad + 4, :].rearrange("g q n -> q g n").bitcast(I32),
             )
-        nc.sync.dma_start(out=rows[0:1, 0:D], in_=b1.rearrange("(o n) -> o n", o=1))
-        for half in range(2):
-            nc.sync.dma_start(out=w1_w[:, half, :].bitcast(I32), in_=w1_words[half].bitcast(I32))
-        nc.sync.dma_start(out=rows[0:1, D : 2 * D], in_=g.rearrange("(o n) -> o n", o=1))
-        nc.sync.dma_start(out=rows[0:1, 2 * D : 2 * D + C], in_=bo.rearrange("(o n) -> o n", o=1))
-        nc.sync.dma_start(out=g2_cols[:], in_=g[F : 2 * F].rearrange("(p t) -> p t", t=PACK))
         for quad in range(4):
             nc.sync.dma_start(
                 out=wo_s[32 * quad : 32 * quad + 4, :, :].bitcast(I32),
                 in_=wo_scales[:, 4 * quad : 4 * quad + 4, :].rearrange("g q n -> q g n").bitcast(I32),
             )
         nc.sync.dma_start(out=wo_w[:].bitcast(I32), in_=wo_words.rearrange("g p n -> p g n").bitcast(I32))
-
-        s_bf = keep.tile([P, D], BF16, name="s_bf")
-        for blk in range(D // P):
-            cols = slice(blk * P, (blk + 1) * P)
-            if blk < 5:
-                nc.vector.tensor_scalar(
-                    out=s_bf[:, cols], in0=s_u8[:, cols].bitcast(FP8), scalar1=s_sc[:, blk : blk + 1], scalar2=None, op0=ALU.mult
-                )
-            else:
-                nc.scalar.activation(out=s_bf[:, cols], in_=s_u8[:, cols].bitcast(FP8), func=ACT.Copy, scale=s_sc[:, blk : blk + 1])
-        s_words = s_bf[:].bitcast(F32)
-        s_turned = bank(3, "s_turned")
-        for half in range(2):
-            for u in range(2):
-                at = (2 * half + u) * P
-                nc.tensor.transpose(s_turned[:, at : at + P], s_words[:, 256 * half + u : 256 * (half + 1) : 2], ident)
-        s_grp = keep.tile([P, 2 * L * PACK], BF16, name="s_grp", align_bytes=64)
-        nc.vector.tensor_copy(
-            out=s_grp[:].bitcast(F32).rearrange("p (g r u) -> p g r u", g=2, u=2),
-            in_=s_turned[:].rearrange("p (g u r) -> p g r u", g=2, u=2),
-        )
-        nc.vector.tensor_scalar(out=neg_g2[:], in0=g2_cols[:], scalar1=-1.0, scalar2=None, op0=ALU.mult)
-        s_codes = keep.tile([P, 2 * L], U32, name="s_codes", align_bytes=64)
-        s_scales = keep.tile([P, 2 * L], U8, name="s_scales", align_bytes=64)
-        nc.vector.quantize_mx(out=s_codes[:].bitcast(FP8X4), scales=s_scales[:], in_=s_grp[:])
-
-        for turn in range(1, CLASSES):
-            dst = perm[:, turn, :].rearrange("p (b a) -> p b a", a=CLASSES)
-            src = ident.rearrange("p (b a) -> p b a", a=CLASSES)
-            nc.scalar.copy(out=dst[:, :, 0 : CLASSES - turn], in_=src[:, :, turn:CLASSES])
-            nc.scalar.copy(out=dst[:, :, CLASSES - turn : CLASSES], in_=src[:, :, 0:turn])
 
         def spread(index, name, first):
             spread_bank = bank(index, name)
@@ -157,10 +126,43 @@ def tile_esmfoldsequencetopairproductdifference_d1p_kernel(
             )
             return spread_bank
 
+        s_bf = keep.tile([P, D], BF16, name="s_bf")
+        for blk in range(D // P):
+            cols = slice(blk * P, (blk + 1) * P)
+            if blk < 5:
+                nc.vector.tensor_scalar(
+                    out=s_bf[:, cols], in0=s_u8[:, cols].bitcast(FP8), scalar1=s_sc[:, blk : blk + 1], scalar2=None, op0=ALU.mult
+                )
+            else:
+                nc.scalar.activation(out=s_bf[:, cols], in_=s_u8[:, cols].bitcast(FP8), func=ACT.Copy, scale=s_sc[:, blk : blk + 1])
+        s_words = s_bf[:].bitcast(F32)
+        s_grp = keep.tile([P, 2, L * PACK], BF16, name="s_grp", align_bytes=64)
+        for ps in range(2):
+            s_turned = bank(3 + 3 * ps, "s_turned%d" % ps)
+            for u in range(2):
+                nc.tensor.transpose(s_turned[:, u * P : (u + 1) * P], s_words[:, 256 * ps + u : 256 * (ps + 1) : 2], ident)
+            nc.vector.tensor_copy(
+                out=s_grp[:, ps, :].bitcast(F32).rearrange("p (r u) -> p r u", u=2),
+                in_=s_turned[:, 0 : 2 * P].rearrange("p (u r) -> p r u", u=2),
+            )
+        s_codes = keep.tile([P, 2, L], U32, name="s_codes", align_bytes=64)
+        s_scales = keep.tile([P, 2, L], U8, name="s_scales", align_bytes=64)
+        for ps in range(2):
+            nc.vector.quantize_mx(out=s_codes[:, ps, :].bitcast(FP8X4), scales=s_scales[:, ps, :], in_=s_grp[:, ps, :])
+
+        b1_banks = [spread(4 + half, "b1_bank%d" % half, half * F) for half in range(2)]
         b1_sb = keep.tile([P, 2, F], F32, name="b1_sb")
         for half in range(2):
-            b1_bank = spread(4 + half, "b1_bank%d" % half, half * F)
-            nc.scalar.copy(out=b1_sb[:, half, :], in_=b1_bank[:])
+            nc.scalar.copy(out=b1_sb[:, half, :], in_=b1_banks[half][:])
+        g2_bank = spread(7, "g2_bank", D)
+        neg_g2_sb = keep.tile([P, F], F32, name="neg_g2_sb")
+        nc.scalar.activation(out=neg_g2_sb[:], in_=g2_bank[:], func=ACT.Copy, scale=-1.0)
+        for turn in range(1, CLASSES):
+            dst = perm[:, turn, :].rearrange("p (b a) -> p b a", a=CLASSES)
+            src = ident.rearrange("p (b a) -> p b a", a=CLASSES)
+            nc.scalar.copy(out=dst[:, :, 0 : CLASSES - turn], in_=src[:, :, turn:CLASSES])
+            nc.scalar.copy(out=dst[:, :, CLASSES - turn : CLASSES], in_=src[:, :, 0:turn])
+        nc.gpsimd.tensor_scalar(out=neg_g2[:], in0=g_cols[:, 1, :], scalar1=-1.0, scalar2=0.0, op0=ALU.mult, op1=ALU.add)
 
         h_banks = []
         for half in range(2):
@@ -168,24 +170,22 @@ def tile_esmfoldsequencetopairproductdifference_d1p_kernel(
             for ps in range(2):
                 nc.tensor.matmul_mx(
                     out=h_bank[:],
-                    lhsT=s_codes[:, ps * L : (ps + 1) * L].bitcast(FP8X4),
-                    lhsT_scale=s_scales[:, ps * L : (ps + 1) * L],
+                    lhsT=s_codes[:, ps, :].bitcast(FP8X4),
+                    lhsT_scale=s_scales[:, ps, :],
                     rhs=w1_w[:, ps, half * 2 * F : (half + 1) * 2 * F].bitcast(FP4X4),
                     rhs_scale=w1_s[:, ps, half * F : (half + 1) * F],
                     start=(ps == 0),
                     stop=(ps == 1),
                 )
             h_banks.append(h_bank)
-        g1_bank = spread(6, "g1_bank", D)
-        g2_bank = spread(7, "g2_bank", D + F)
+
         bo_bank = bank(0, "bo_bank")
-        nc.tensor.matmul(out=bo_bank[:, 0:C], lhsT=ones[:], rhs=rows[:, 2 * D : 2 * D + C], start=True, stop=True)
+        nc.tensor.matmul(out=bo_bank[:, 0:C], lhsT=ones[:], rhs=rows[:, D + F : D + F + C], start=True, stop=True)
         bo_sb = keep.tile([P, C], F32, name="bo_sb")
         nc.scalar.copy(out=bo_sb[:], in_=bo_bank[:, 0:C])
 
         q_tok = keep.tile([P, F], F32, name="q_tok")
         k_tok = keep.tile([P, F], F32, name="k_tok")
-        qg1_tok = keep.tile([P, F], F32, name="qg1_tok")
         qg2_tok = keep.tile([P, F], F32, name="qg2_tok")
         nkg2_tok = keep.tile([P, F], F32, name="nkg2_tok")
         for half, dst in enumerate((q_tok, k_tok)):
@@ -195,26 +195,22 @@ def tile_esmfoldsequencetopairproductdifference_d1p_kernel(
                 in1=b1_sb[:, half, :].rearrange("i (t p) -> i t p", t=PACK),
                 op=ALU.add,
             )
-        nc.vector.tensor_tensor(out=qg1_tok[:], in0=q_tok[:], in1=g1_bank[:], op=ALU.mult)
         nc.vector.tensor_tensor(out=qg2_tok[:], in0=q_tok[:], in1=g2_bank[:], op=ALU.mult)
-        nc.vector.scalar_tensor_tensor(out=nkg2_tok[:], in0=k_tok[:], scalar=-1.0, in1=g2_bank[:], op0=ALU.mult, op1=ALU.mult)
+        nc.gpsimd.tensor_tensor(out=nkg2_tok[:], in0=k_tok[:], in1=neg_g2_sb[:], op=ALU.mult)
         parked = out[:, PARK : PARK + PACK, :].rearrange("i j c -> i (j c)")
         nc.sync.dma_start(out=parked, in_=qg2_tok[:])
 
-        def turn_tokens(index, name, src, interleave):
+        def turn_tokens(index, name, src):
             turned = bank(index, name)
             for t in range(PACK):
-                if interleave:
-                    dst = turned[:].rearrange("p (n t) -> p n t", t=PACK)[:, :, t]
-                else:
-                    dst = turned[:, t * P : (t + 1) * P]
+                dst = turned[:].rearrange("p (n t) -> p n t", t=PACK)[:, :, t]
                 nc.tensor.transpose(dst, src[:, t * P : (t + 1) * P], ident)
             return turned
 
-        k_bank = turn_tokens(0, "k_bank", k_tok, True)
-        qg1_bank = turn_tokens(3, "qg1_bank", qg1_tok, False)
-        qg2_bank = turn_tokens(4, "qg2_bank", qg2_tok, False)
-        nkg2_bank = turn_tokens(5, "nkg2_bank", nkg2_tok, True)
+        q_bank = turn_tokens(3, "q_bank", q_tok)
+        k_bank = turn_tokens(0, "k_bank", k_tok)
+        qg2_bank = turn_tokens(4, "qg2_bank", qg2_tok)
+        nkg2_bank = turn_tokens(5, "nkg2_bank", nkg2_tok)
 
         k_sb = keep.tile([P, F], F32, name="k_sb")
         k_planes = keep.tile([P, PACK, L], F32, name="k_planes")
@@ -222,20 +218,22 @@ def tile_esmfoldsequencetopairproductdifference_d1p_kernel(
         qg2 = keep.tile([P, L, PACK], F32, name="qg2")
         nc.scalar.copy(out=k_sb[:], in_=k_bank[:])
         nc.scalar.copy(out=k_planes[:], in_=k_bank[:].rearrange("p (n t) -> p t n", t=PACK))
-        nc.vector.tensor_copy(
+        nc.vector.tensor_tensor(
             out=qg1[:, :, 0:16].rearrange("p r (a t) -> p r a t", t=PACK),
-            in_=qg1_bank[:].rearrange("p (t a r) -> p r a t", t=PACK, a=CLASSES),
+            in0=q_bank[:].rearrange("p (a r t) -> p r a t", t=PACK, a=CLASSES),
+            in1=g_cols[:, 0, :].unsqueeze(1).unsqueeze(1).to_broadcast([P, SPAN, CLASSES, PACK]),
+            op=ALU.mult,
         )
-        nc.scalar.copy(out=qg2[:], in_=qg2_bank[:].rearrange("p (t j) -> p j t", t=PACK))
-        nc.scalar.copy(out=qg1[:, :, 16:28], in_=qg1[:, :, 0:12])
+        nc.scalar.copy(out=qg2[:].rearrange("p j t -> p (j t)"), in_=qg2_bank[:])
 
         q_rep = [keep.tile([P, RUN, F], F32, name="q_rep%d" % block) for block in range(BLOCKS)]
 
-        def load_replicas(block):
+        def load_replicas(block, lo, hi):
             for a in range(CLASSES):
                 first = SPAN * a + RUN * block
                 nc.sync.dma_start(
-                    out=q_rep[block][a:P:CLASSES, :, :], in_=parked[first : first + RUN, :].partition_broadcast(SPAN)
+                    out=q_rep[block][a:P:CLASSES, lo:hi, :],
+                    in_=parked[first + lo : first + hi, :].partition_broadcast(SPAN),
                 )
 
         c_scalar, c_vector, codes, results = {}, {}, {}, {}
@@ -410,14 +408,17 @@ def tile_esmfoldsequencetopairproductdifference_d1p_kernel(
             result = work.tile([P, 8, C], F32, name="result", tag="result", bufs=3)
             results[m] = (acc, result)
 
-        load_replicas(0)
+        load_replicas(0, 0, RUN // 2)
+        load_replicas(0, RUN // 2, RUN)
         scalar_work(0)
         for m in range(len(groups)):
             vector_work(m)
             if 1 <= m < BLOCKS:
-                load_replicas(m)
+                load_replicas(m, 0, RUN)
             if m + 1 < len(groups):
                 scalar_work(m + 1)
+            if m == 0:
+                nc.vector.tensor_copy(out=qg1[:, :, 16:28], in_=qg1[:, :, 0:12])
             quantise(m)
             multiply(m)
         last = len(groups) - 1

@@ -24,7 +24,6 @@ SPAN = L // CLASSES
 RUN = 6
 BLOCKS = 4
 PARK = 124
-GPSIMD_ROWS = 12
 
 
 def plan():
@@ -34,8 +33,10 @@ def plan():
     ]
     singles = [28, 29, 30, 31] + list(range(88, 96)) + [120, 121, 122, 123]
     for m in range(BLOCKS * CLASSES):
-        groups.append(dict_group(m // CLASSES, m % CLASSES, [singles[m]], 1 if m % 3 == 2 else 0, 0, GPSIMD_ROWS))
-    groups.append(dict_group(None, None, [124, 125, 126, 127], 0, 0, 12))
+        groups.append(dict_group(m // CLASSES, m % CLASSES, [singles[m]], 0 if m % 3 == 0 else 1, 0, 15 if m % 3 == 0 else 13))
+    groups.append(dict_group(None, None, [124, 125, 126, 127], 2, 0, 10))
+    for m, grp in enumerate(groups):
+        place(m, grp)
     return groups
 
 
@@ -43,11 +44,24 @@ def dict_group(block, turn, fixed, s_prods, v_diffs, g_rows):
     shifted = 0 if block is None else RUN
     units = shifted + len(fixed)
     on_scalar = [("diff", u) for u in range(units - v_diffs)] + [("prod", u) for u in range(units - s_prods, units)]
-    on_vector = [("prod", u) for u in range(units - s_prods)] + [("diff", u) for u in range(units - v_diffs, units)]
+    shared = [("prod", u) for u in range(shifted if shifted else units - s_prods)]
+    alone = [("prod", u) for u in range(len(shared), units - s_prods)] + [("diff", u) for u in range(units - v_diffs, units)]
     return {
         "block": block, "turn": turn, "fixed": fixed, "shifted": shifted, "units": units,
-        "s_prods": s_prods, "v_diffs": v_diffs, "g_rows": g_rows, "on_scalar": on_scalar, "on_vector": on_vector,
+        "s_prods": s_prods, "v_diffs": v_diffs, "g_rows": g_rows, "on_scalar": on_scalar, "shared": shared, "alone": alone,
     }
+
+
+def place(m, grp):
+    if m % 2 == 0:
+        halves = grp["on_scalar"] + grp["alone"] + grp["shared"]
+        first = 8 - len(grp["on_scalar"])
+    else:
+        halves = grp["shared"] + grp["alone"] + grp["on_scalar"]
+        first = max(8, 15 - len(grp["shared"]) - len(grp["alone"]))
+    grp.setdefault("first", first)
+    grp.setdefault("halves", halves)
+    grp.setdefault("slot", {half: first + at for at, half in enumerate(halves)})
 
 
 def power_of_two_runs(count):
@@ -236,27 +250,33 @@ def tile_esmfoldsequencetopairproductdifference_d1p_kernel(
                     in_=parked[first + lo : first + hi, :].partition_broadcast(SPAN),
                 )
 
-        c_scalar, c_vector, codes, results = {}, {}, {}, {}
+        codes, results = {}, {}
+        c_all = keep.tile([P, 24, F], BF16, name="c_all", align_bytes=64)
         diff_banks = [3, 4, 6, 7, 5]
         diff_count = [0]
 
-        def fixed_on_scalar(kind, j, dst):
-            planes = work.tile([P, PACK, L], BF16, name="planes", tag="planes", bufs=3)
-            for t in range(PACK):
-                if kind == "diff":
-                    nc.scalar.activation(
-                        out=planes[:, t, :], in_=k_planes[:, t, :], func=ACT.Identity,
-                        scale=neg_g2[:, t : t + 1], bias=qg2[:, j, t : t + 1],
-                    )
-                else:
-                    at = PACK * (j // SPAN) + t
-                    nc.scalar.activation(
-                        out=planes[:, t, :], in_=k_planes[:, t, :], func=ACT.Copy, scale=qg1[:, j % SPAN, at : at + 1]
-                    )
+        def fixed_on_scalar(grp, halves):
+            count = len(halves)
+            planes = work.tile([P, PACK, count * L], BF16, name="planes", tag="planes")
+            for at, (kind, u) in enumerate(halves):
+                j = grp["fixed"][u - grp["shifted"]]
+                for t in range(PACK):
+                    dst = planes[:, t, at * L : (at + 1) * L]
+                    if kind == "diff":
+                        nc.scalar.activation(
+                            out=dst, in_=k_planes[:, t, :], func=ACT.Identity,
+                            scale=neg_g2[:, t : t + 1], bias=qg2[:, j, t : t + 1],
+                        )
+                    else:
+                        col = PACK * (j // SPAN) + t
+                        nc.scalar.activation(
+                            out=dst, in_=k_planes[:, t, :], func=ACT.Copy, scale=qg1[:, j % SPAN, col : col + 1]
+                        )
+            slot = grp["slot"][halves[0]]
 
             def interleave():
                 nc.scalar.copy(
-                    out=dst.rearrange("p (c i t) -> p c t i", i=4, t=PACK),
+                    out=c_all[:, slot : slot + count, :].rearrange("p u (c i t) -> p (u c) t i", i=4, t=PACK),
                     in_=planes[:].rearrange("p t (c i) -> p c t i", i=4),
                 )
 
@@ -281,25 +301,25 @@ def tile_esmfoldsequencetopairproductdifference_d1p_kernel(
 
         def scalar_work(m):
             grp = groups[m]
-            tile = work.tile([P, 8, F], BF16, name="c_scalar", tag="c_scalar", align_bytes=64)
-            c_scalar[m] = tile
-            slots = list(enumerate(grp["on_scalar"]))
-            ahead = min(2, grp["shifted"])
-            slots = slots[:ahead] + slots[grp["shifted"] :] + slots[ahead : grp["shifted"]]
+            shifted = grp["shifted"]
+            fixed = grp["on_scalar"][shifted:]
+            steps = [fixed[at : at + 2] for at in range(0, len(fixed), 2)]
+            ahead = min(2, shifted)
+            steps = list(range(ahead)) + steps + list(range(ahead, shifted))
             pending = None
-            for slot, (kind, u) in slots:
+            for step in steps:
                 following = None
-                if u < grp["shifted"]:
-                    shifted_diff(grp, u, tile[:, slot, :])
+                if isinstance(step, int):
+                    shifted_diff(grp, step, c_all[:, grp["slot"][("diff", step)], :])
                 else:
-                    following = fixed_on_scalar(kind, grp["fixed"][u - grp["shifted"]], tile[:, slot, :])
+                    following = fixed_on_scalar(grp, step)
                 if pending is not None:
                     pending()
                 pending = following
             if pending is not None:
                 pending()
 
-        def products(engine, k_src, grp, tile, first, count, row0, row1):
+        def products(engine, k_src, grp, first, count, row0, row1):
             lo, hi = 16 * row0, 16 * row1
             if first < grp["shifted"]:
                 inner = 16
@@ -311,8 +331,9 @@ def tile_esmfoldsequencetopairproductdifference_d1p_kernel(
                 tau = j % SPAN
                 at = PACK * (j // SPAN)
             shape = [P, count, (hi - lo) // inner, inner]
+            slot = grp["slot"][("prod", first)]
             engine.tensor_tensor(
-                out=tile[:, first : first + count, lo:hi].rearrange("p u (b x) -> p u b x", x=inner),
+                out=c_all[:, slot : slot + count, lo:hi].rearrange("p u (b x) -> p u b x", x=inner),
                 in0=k_src[:, lo:hi].rearrange("p (b x) -> p b x", x=inner).unsqueeze(1).to_broadcast(shape),
                 in1=qg1[:, tau : tau + count, at : at + inner].unsqueeze(2).to_broadcast(shape),
                 op=ALU.mult,
@@ -345,50 +366,45 @@ def tile_esmfoldsequencetopairproductdifference_d1p_kernel(
 
         def vector_work(m):
             grp = groups[m]
-            tile = work.tile([P, 11, F], BF16, name="c_vector", tag="c_vector", bufs=1, align_bytes=64)
-            c_vector[m] = tile
-            shared = grp["shifted"] if grp["shifted"] else grp["units"]
+            shared = len(grp["shared"])
             split = SPAN - grp["g_rows"]
-            products(nc.gpsimd, k_sb, grp, tile, 0, shared, split, SPAN)
-            products(nc.vector, k_bank, grp, tile, 0, shared // 2, 0, split)
-            if m:
-                evacuate(m - 1, 0)
-            products(nc.vector, k_bank, grp, tile, shared // 2, shared // 2, 0, split)
-            if m:
-                evacuate(m - 1, 1)
-                store(m - 1)
+            products(nc.gpsimd, k_sb, grp, 0, shared, split, SPAN)
+            products(nc.vector, k_bank, grp, 0, shared, 0, split)
             if grp["shifted"] and not grp["s_prods"]:
-                products(nc.vector, k_bank, grp, tile, shared, 1, 0, SPAN)
+                products(nc.vector, k_bank, grp, shared, 1, 0, SPAN)
             if grp["v_diffs"]:
                 count = grp["v_diffs"]
                 j = grp["fixed"][grp["units"] - count]
+                slot = grp["slot"][("diff", grp["units"] - count)]
                 shape = [P, count, L, PACK]
                 nc.vector.tensor_tensor(
-                    out=tile[:, grp["units"] : grp["units"] + count, :].rearrange("p u (n t) -> p u n t", t=PACK),
+                    out=c_all[:, slot : slot + count, :].rearrange("p u (n t) -> p u n t", t=PACK),
                     in0=nkg2_bank[:].rearrange("p (n t) -> p n t", t=PACK).unsqueeze(1).to_broadcast(shape),
                     in1=qg2[:, j : j + count, :].unsqueeze(2).to_broadcast(shape),
                     op=ALU.add,
                 )
+            if m:
+                evacuate(m - 1, 0)
+                evacuate(m - 1, 1)
+                store(m - 1)
 
         def quantise(m):
             grp = groups[m]
-            where = {}
-            for name, tile, halves, most in (
-                ("s", c_scalar[m], grp["on_scalar"], 8), ("v", c_vector[m], grp["on_vector"], 11)
-            ):
-                words = work.tile([P, most * L], U32, name="words_" + name, tag="words_" + name, align_bytes=64)
-                scales = work.tile([P, most * L], U8, name="scales_" + name, tag="scales_" + name, align_bytes=64)
-                for start, width in power_of_two_runs(len(halves)):
-                    cols = slice(start * L, (start + width) * L)
-                    nc.vector.quantize_mx(
-                        out=words[:, cols].bitcast(FP8X4),
-                        scales=scales[:, cols],
-                        in_=tile[:, start : start + width, :].rearrange("p u x -> p (u x)"),
-                    )
-                for slot, half in enumerate(halves):
-                    cols = slice(slot * L, (slot + 1) * L)
-                    where[half] = (words[:, cols], scales[:, cols])
-            codes[m] = where
+            count, first = len(grp["halves"]), grp["first"]
+            words = work.tile([P, 16 * L], U32, name="words", tag="words", align_bytes=64)
+            scales = work.tile([P, 16 * L], U8, name="scales", tag="scales", align_bytes=64)
+            for start, width in power_of_two_runs(count):
+                at = start if m % 2 == 0 else count - start - width
+                cols = slice(at * L, (at + width) * L)
+                nc.vector.quantize_mx(
+                    out=words[:, cols].bitcast(FP8X4),
+                    scales=scales[:, cols],
+                    in_=c_all[:, first + at : first + at + width, :].rearrange("p u x -> p (u x)"),
+                )
+            codes[m] = {
+                half: (words[:, at * L : (at + 1) * L], scales[:, at * L : (at + 1) * L])
+                for at, half in enumerate(grp["halves"])
+            }
 
         def multiply(m):
             grp = groups[m]

@@ -21,27 +21,36 @@ P = 128
 PACK = 4
 CLASSES = 4
 SPAN = L // CLASSES
-RUN = 6
-BLOCKS = 4
+RUNS = (7, 6, 6, 6)
+STARTS = (0, 7, 13, 19)
 PARK = 124
+ON_VECTOR = (2,)
+MIXED = 3
 
 
 def plan():
     groups = [
-        dict_group(None, None, [24, 25, 26, 27], 0, 2, 14),
-        dict_group(None, None, list(range(56, 64)), 0, 3, 16),
+        dict_group(None, None, list(range(25, 30)), 0, 3, 16),
+        dict_group(None, None, list(range(57, 64)), 0, 2, 15),
     ]
-    singles = [28, 29, 30, 31] + list(range(88, 96)) + [120, 121, 122, 123]
-    for m in range(BLOCKS * CLASSES):
-        groups.append(dict_group(m // CLASSES, m % CLASSES, [singles[m]], 0 if m % 3 == 0 else 1, 0, 15 if m % 3 == 0 else 13))
+    singles = [30, 31] + list(range(89, 96)) + [121, 122, 123]
+    short = 0
+    for m in range(len(RUNS) * CLASSES):
+        if m % CLASSES == 0:
+            groups.append(dict_group(0, m // CLASSES, [], 0, 0, 32))
+        else:
+            s_prods = 0 if m in ON_VECTOR else 1
+            groups.append(dict_group(1 + short // CLASSES, short % CLASSES, [singles[short]], s_prods, 0, 27 if s_prods else 32))
+            short += 1
     groups.append(dict_group(None, None, [124, 125, 126, 127], 2, 0, 10))
     for m, grp in enumerate(groups):
         place(m, grp)
+        grp.setdefault("per_bank", 2 if m == len(groups) - 1 else 4)
     return groups
 
 
 def dict_group(block, turn, fixed, s_prods, v_diffs, g_rows):
-    shifted = 0 if block is None else RUN
+    shifted = 0 if block is None else RUNS[block]
     units = shifted + len(fixed)
     on_scalar = [("diff", u) for u in range(units - v_diffs)] + [("prod", u) for u in range(units - s_prods, units)]
     shared = [("prod", u) for u in range(shifted if shifted else units - s_prods)]
@@ -55,7 +64,7 @@ def dict_group(block, turn, fixed, s_prods, v_diffs, g_rows):
 def place(m, grp):
     if m % 2 == 0:
         halves = grp["on_scalar"] + grp["alone"] + grp["shared"]
-        first = 8 - len(grp["on_scalar"])
+        first = min(8 - len(grp["on_scalar"]), 15 - len(halves))
     else:
         halves = grp["shared"] + grp["alone"] + grp["on_scalar"]
         first = max(8, 15 - len(grp["shared"]) - len(grp["alone"]))
@@ -101,32 +110,30 @@ def tile_esmfoldsequencetopairproductdifference_d1p_kernel(
         perm = keep.tile([P, CLASSES, P], F32, name="perm")
         warm = keep.tile([P, 1], F32, name="warm")
 
-        nc.vector.memset(rows[:].bitcast(I32), 0)
         nc.vector.memset(w1_s[:].rearrange("p g n -> p (g n)").bitcast(I32), 0)
+        nc.vector.memset(rows[:].bitcast(I32), 0)
         nc.vector.memset(wo_s[:].rearrange("p g n -> p (g n)").bitcast(I32), 0)
         nc.gpsimd.memset(ones[:], 1.0)
         make_identity(nc, perm[:, 0, :])
         ident = perm[:, 0, :]
         nc.scalar.activation(out=warm[:], in_=ones[:, 0:1], func=ACT.Identity)
 
+        def load_scales(plane, scale_rows):
+            for quad in range(4):
+                nc.sync.dma_start(
+                    out=plane[32 * quad : 32 * quad + 4, :, :].bitcast(I32),
+                    in_=scale_rows[:, 4 * quad : 4 * quad + 4, :].rearrange("g q n -> q g n").bitcast(I32),
+                )
+
         nc.sync.dma_start(out=s_u8[:], in_=s_bytes)
         nc.sync.dma_start(out=s_sc[:], in_=s_scale)
+        load_scales(w1_s, w1_scales)
         nc.sync.dma_start(out=rows[0:1, 0:D], in_=b1.rearrange("(o n) -> o n", o=1))
+        nc.sync.dma_start(out=w1_w[:].bitcast(I32), in_=w1_words.rearrange("g p n -> p g n").bitcast(I32))
         nc.sync.dma_start(out=rows[0:1, D : D + F], in_=g[F : 2 * F].rearrange("(o n) -> o n", o=1))
-        nc.sync.dma_start(out=rows[0:1, D + F : D + F + C], in_=bo.rearrange("(o n) -> o n", o=1))
-        for half in range(2):
-            nc.sync.dma_start(out=w1_w[:, half, :].bitcast(I32), in_=w1_words[half].bitcast(I32))
         nc.sync.dma_start(out=g_cols[:], in_=g.rearrange("(h p t) -> p h t", h=2, t=PACK))
-        for quad in range(4):
-            nc.sync.dma_start(
-                out=w1_s[32 * quad : 32 * quad + 4, :, :].bitcast(I32),
-                in_=w1_scales[:, 4 * quad : 4 * quad + 4, :].rearrange("g q n -> q g n").bitcast(I32),
-            )
-        for quad in range(4):
-            nc.sync.dma_start(
-                out=wo_s[32 * quad : 32 * quad + 4, :, :].bitcast(I32),
-                in_=wo_scales[:, 4 * quad : 4 * quad + 4, :].rearrange("g q n -> q g n").bitcast(I32),
-            )
+        nc.sync.dma_start(out=rows[0:1, D + F : D + F + C], in_=bo.rearrange("(o n) -> o n", o=1))
+        load_scales(wo_s, wo_scales)
         nc.sync.dma_start(out=wo_w[:].bitcast(I32), in_=wo_words.rearrange("g p n -> p g n").bitcast(I32))
 
         def spread(index, name, first):
@@ -240,11 +247,11 @@ def tile_esmfoldsequencetopairproductdifference_d1p_kernel(
         )
         nc.scalar.copy(out=qg2[:].rearrange("p j t -> p (j t)"), in_=qg2_bank[:])
 
-        q_rep = [keep.tile([P, RUN, F], F32, name="q_rep%d" % block) for block in range(BLOCKS)]
+        q_rep = [keep.tile([P, run, F], F32, name="q_rep%d" % block) for block, run in enumerate(RUNS)]
 
         def load_replicas(block, lo, hi):
             for a in range(CLASSES):
-                first = SPAN * a + RUN * block
+                first = SPAN * a + STARTS[block]
                 nc.sync.dma_start(
                     out=q_rep[block][a:P:CLASSES, lo:hi, :],
                     in_=parked[first + lo : first + hi, :].partition_broadcast(SPAN),
@@ -323,7 +330,7 @@ def tile_esmfoldsequencetopairproductdifference_d1p_kernel(
             lo, hi = 16 * row0, 16 * row1
             if first < grp["shifted"]:
                 inner = 16
-                tau = RUN * grp["block"] + first
+                tau = STARTS[grp["block"]] + first
                 at = PACK * grp["turn"]
             else:
                 inner = PACK
@@ -341,12 +348,13 @@ def tile_esmfoldsequencetopairproductdifference_d1p_kernel(
 
         def evacuate(m, half):
             grp = groups[m]
-            count = min(4, grp["units"] - 4 * half)
+            per_bank = grp["per_bank"]
+            count = min(per_bank, grp["units"] - per_bank * half)
             if count <= 0:
                 return
             acc, result = results[m]
             nc.vector.tensor_tensor(
-                out=result[:, 4 * half : 4 * half + count, :],
+                out=result[:, per_bank * half : per_bank * half + count, :],
                 in0=acc[half][:, 0 : count * C].rearrange("p (u c) -> p u c", c=C),
                 in1=bo_sb[:].unsqueeze(1).to_broadcast([P, count, C]),
                 op=ALU.add,
@@ -358,19 +366,28 @@ def tile_esmfoldsequencetopairproductdifference_d1p_kernel(
             shifted = grp["shifted"]
             if shifted:
                 for a in range(CLASSES):
-                    j = SPAN * ((a + grp["turn"]) % CLASSES) + RUN * grp["block"]
-                    nc.sync.dma_start(out=out[a:L:CLASSES, j : j + RUN, :], in_=result[a:P:CLASSES, 0:RUN, :])
-            j = grp["fixed"][0]
-            count = len(grp["fixed"])
-            nc.sync.dma_start(out=out[:, j : j + count, :], in_=result[:, shifted : shifted + count, :])
+                    j = SPAN * ((a + grp["turn"]) % CLASSES) + STARTS[grp["block"]]
+                    nc.sync.dma_start(out=out[a:L:CLASSES, j : j + shifted, :], in_=result[a:P:CLASSES, 0:shifted, :])
+            if grp["fixed"]:
+                j = grp["fixed"][0]
+                count = len(grp["fixed"])
+                nc.sync.dma_start(out=out[:, j : j + count, :], in_=result[:, shifted : shifted + count, :])
 
         def vector_work(m):
             grp = groups[m]
             shared = len(grp["shared"])
             split = SPAN - grp["g_rows"]
-            products(nc.gpsimd, k_sb, grp, 0, shared, split, SPAN)
-            products(nc.vector, k_bank, grp, 0, shared, 0, split)
-            if grp["shifted"] and not grp["s_prods"]:
+            if grp["shifted"]:
+                whole = shared - MIXED
+                mixed = whole if m % 2 == 0 else 0
+                products(nc.gpsimd, k_sb, grp, mixed, MIXED, split, SPAN)
+                products(nc.vector, k_bank, grp, 0 if m % 2 == 0 else MIXED, whole, 0, SPAN)
+                if split:
+                    products(nc.vector, k_bank, grp, mixed, MIXED, 0, split)
+            else:
+                products(nc.gpsimd, k_sb, grp, 0, shared, split, SPAN)
+                products(nc.vector, k_bank, grp, 0, shared, 0, split)
+            if grp["shifted"] and grp["alone"]:
                 products(nc.vector, k_bank, grp, shared, 1, 0, SPAN)
             if grp["v_diffs"]:
                 count = grp["v_diffs"]
@@ -408,12 +425,13 @@ def tile_esmfoldsequencetopairproductdifference_d1p_kernel(
 
         def multiply(m):
             grp = groups[m]
-            acc = [bank(1 + half, "acc%d" % half) for half in range((grp["units"] + 3) // 4)]
+            per_bank = grp["per_bank"]
+            acc = [bank(1 + half, "acc%d" % half) for half in range(-(-grp["units"] // per_bank))]
             for u in range(grp["units"]):
                 for ps, kind in enumerate(("prod", "diff")):
                     words, scales = codes[m][(kind, u)]
                     nc.tensor.matmul_mx(
-                        out=acc[u // 4][:, (u % 4) * C : (u % 4 + 1) * C],
+                        out=acc[u // per_bank][:, (u % per_bank) * C : (u % per_bank + 1) * C],
                         lhsT=words.bitcast(FP8X4),
                         lhsT_scale=scales,
                         rhs=wo_w[:, ps, :].bitcast(FP4X4),
@@ -424,13 +442,13 @@ def tile_esmfoldsequencetopairproductdifference_d1p_kernel(
             result = work.tile([P, 8, C], F32, name="result", tag="result", bufs=3)
             results[m] = (acc, result)
 
-        load_replicas(0, 0, RUN // 2)
-        load_replicas(0, RUN // 2, RUN)
+        load_replicas(0, 0, 3)
+        load_replicas(0, 3, RUNS[0])
         scalar_work(0)
         for m in range(len(groups)):
             vector_work(m)
-            if 1 <= m < BLOCKS:
-                load_replicas(m, 0, RUN)
+            if m + 1 < len(RUNS):
+                load_replicas(m + 1, 0, RUNS[m + 1])
             if m + 1 < len(groups):
                 scalar_work(m + 1)
             if m == 0:
@@ -438,6 +456,7 @@ def tile_esmfoldsequencetopairproductdifference_d1p_kernel(
             quantise(m)
             multiply(m)
         last = len(groups) - 1
-        evacuate(last, 0)
-        evacuate(last, 1)
-        store(last)
+        for half in range(2):
+            evacuate(last, half)
+            j = groups[last]["fixed"][2 * half]
+            nc.sync.dma_start(out=out[:, j : j + 2, :], in_=results[last][1][:, 2 * half : 2 * half + 2, :])

from contextlib import ExitStack

import concourse.mybir as mybir
from concourse.masks import make_identity

L, D, F, C = 128, 1024, 512, 128
FLOPS = 2 * L * D * 2 * F + 2 * L * L * 2 * F * C

F32 = mybir.dt.float32
BF16 = mybir.dt.bfloat16
I32 = mybir.dt.int32
U32 = mybir.dt.uint32
U8 = mybir.dt.uint8
FP8 = mybir.dt.float8_e4m3fn
FP8X4 = mybir.dt.float8_e4m3fn_x4
FP4X4 = mybir.dt.float4_e2m1fn_x4
ALU = mybir.AluOpType
ACT = mybir.ActivationFunctionType

P = 128
PACK = 4
CLASSES = 4
SPAN = L // CLASSES
RUNS = (7, 6, 6, 6)
STARTS = (0, 7, 13, 19)
PARK = 124
ON_VECTOR = (2,)
MIXED = 3


def plan():
    groups = [
        dict_group(None, None, list(range(25, 30)), 0, 3, 16),
        dict_group(None, None, list(range(57, 64)), 0, 2, 15),
    ]
    singles = [30, 31] + list(range(89, 96)) + [121, 122, 123]
    short = 0
    for m in range(len(RUNS) * CLASSES):
        if m % CLASSES == 0:
            groups.append(dict_group(0, m // CLASSES, [], 0, 0, 32))
        else:
            s_prods = 0 if m in ON_VECTOR else 1
            groups.append(dict_group(1 + short // CLASSES, short % CLASSES, [singles[short]], s_prods, 0, 27 if s_prods else 32))
            short += 1
    groups.append(dict_group(None, None, [124, 125, 126, 127], 2, 0, 10))
    for m, grp in enumerate(groups):
        place(m, grp)
        grp.setdefault("per_bank", 2 if m == len(groups) - 1 else 4)
    return groups


def dict_group(block, turn, fixed, s_prods, v_diffs, g_rows):
    shifted = 0 if block is None else RUNS[block]
    units = shifted + len(fixed)
    on_scalar = [("diff", u) for u in range(units - v_diffs)] + [("prod", u) for u in range(units - s_prods, units)]
    shared = [("prod", u) for u in range(shifted if shifted else units - s_prods)]
    alone = [("prod", u) for u in range(len(shared), units - s_prods)] + [("diff", u) for u in range(units - v_diffs, units)]
    return {
        "block": block, "turn": turn, "fixed": fixed, "shifted": shifted, "units": units,
        "s_prods": s_prods, "v_diffs": v_diffs, "g_rows": g_rows, "on_scalar": on_scalar, "shared": shared, "alone": alone,
    }


def place(m, grp):
    if m % 2 == 0:
        halves = grp["on_scalar"] + grp["alone"] + grp["shared"]
        first = min(8 - len(grp["on_scalar"]), 15 - len(halves))
    else:
        halves = grp["shared"] + grp["alone"] + grp["on_scalar"]
        first = max(8, 15 - len(grp["shared"]) - len(grp["alone"]))
    grp.setdefault("first", first)
    grp.setdefault("halves", halves)
    grp.setdefault("slot", {half: first + at for at, half in enumerate(halves)})


def power_of_two_runs(count):
    runs, start = [], 0
    for width in (8, 4, 2, 1):
        while count - start >= width:
            runs.append((start, width))
            start += width
    return runs


def tile_esmfoldsequencetopairproductdifference_d1p_kernel(
    tc, s_bytes, s_scale, w1_words, w1_scales, b1, g, wo_words, wo_scales, bo, out
):
    nc = tc.nc
    groups = plan()

    with ExitStack() as ctx:
        keep = ctx.enter_context(tc.tile_pool(name="keep", bufs=1))
        work = ctx.enter_context(tc.tile_pool(name="work", bufs=2))
        psum = ctx.enter_context(tc.psum_pool(name="psum", bufs=1))
        ctx.enter_context(tc.manual_schedule())

        def bank(index, name):
            return psum.tile([P, 512], F32, name=name, tag="bank%d" % index)

        s_u8 = keep.tile([P, D], U8, name="s_u8")
        s_sc = keep.tile([P, D // P], F32, name="s_sc")
        w1_w = keep.tile([P, 2, 2 * D], U8, name="w1_w", align_bytes=64)
        w1_s = keep.tile([P, 2, D], U8, name="w1_s", align_bytes=64)
        wo_w = keep.tile([P, 2, 2 * C], U8, name="wo_w", align_bytes=64)
        wo_s = keep.tile([P, 2, C], U8, name="wo_s", align_bytes=64)
        rows = keep.tile([P, D + F + C], BF16, name="rows")
        g_cols = keep.tile([P, 2, PACK], BF16, name="g_cols")
        neg_g2 = keep.tile([P, PACK], F32, name="neg_g2")
        ones = keep.tile([P, P], BF16, name="ones")
        perm = keep.tile([P, CLASSES, P], F32, name="perm")
        warm = keep.tile([P, 1], F32, name="warm")

        nc.vector.memset(w1_s[:].rearrange("p g n -> p (g n)").bitcast(I32), 0)
        nc.vector.memset(rows[:].bitcast(I32), 0)
        nc.vector.memset(wo_s[:].rearrange("p g n -> p (g n)").bitcast(I32), 0)
        nc.gpsimd.memset(ones[:], 1.0)
        make_identity(nc, perm[:, 0, :])
        ident = perm[:, 0, :]
        nc.scalar.activation(out=warm[:], in_=ones[:, 0:1], func=ACT.Identity)

        def load_scales(plane, scale_rows):
            for quad in range(4):
                nc.sync.dma_start(
                    out=plane[32 * quad : 32 * quad + 4, :, :].bitcast(I32),
                    in_=scale_rows[:, 4 * quad : 4 * quad + 4, :].rearrange("g q n -> q g n").bitcast(I32),
                )

        nc.sync.dma_start(out=s_u8[:], in_=s_bytes)
        nc.sync.dma_start(out=s_sc[:], in_=s_scale)
        load_scales(w1_s, w1_scales)
        nc.sync.dma_start(out=rows[0:1, 0:D], in_=b1.rearrange("(o n) -> o n", o=1))
        nc.sync.dma_start(out=w1_w[:].bitcast(I32), in_=w1_words.rearrange("g p n -> p g n").bitcast(I32))
        nc.sync.dma_start(out=rows[0:1, D : D + F], in_=g[F : 2 * F].rearrange("(o n) -> o n", o=1))
        nc.sync.dma_start(out=g_cols[:], in_=g.rearrange("(h p t) -> p h t", h=2, t=PACK))
        nc.sync.dma_start(out=rows[0:1, D + F : D + F + C], in_=bo.rearrange("(o n) -> o n", o=1))
        load_scales(wo_s, wo_scales)
        nc.sync.dma_start(out=wo_w[:].bitcast(I32), in_=wo_words.rearrange("g p n -> p g n").bitcast(I32))

        def spread(index, name, first):
            spread_bank = bank(index, name)
            nc.tensor.matmul(
                out=spread_bank[:].rearrange("m (t p) -> m t p", t=PACK),
                lhsT=ones[:],
                rhs=rows[:, first : first + F].rearrange("k (p t) -> k t p", t=PACK),
                start=True,
                stop=True,
            )
            return spread_bank

        s_bf = keep.tile([P, D], BF16, name="s_bf")
        for blk in range(D // P):
            cols = slice(blk * P, (blk + 1) * P)
            if blk < 5:
                nc.vector.tensor_scalar(
                    out=s_bf[:, cols], in0=s_u8[:, cols].bitcast(FP8), scalar1=s_sc[:, blk : blk + 1], scalar2=None, op0=ALU.mult
                )
            else:
                nc.scalar.activation(out=s_bf[:, cols], in_=s_u8[:, cols].bitcast(FP8), func=ACT.Copy, scale=s_sc[:, blk : blk + 1])
        s_words = s_bf[:].bitcast(F32)
        s_grp = keep.tile([P, 2, L * PACK], BF16, name="s_grp", align_bytes=64)
        for ps in range(2):
            s_turned = bank(3 + 3 * ps, "s_turned%d" % ps)
            for u in range(2):
                nc.tensor.transpose(s_turned[:, u * P : (u + 1) * P], s_words[:, 256 * ps + u : 256 * (ps + 1) : 2], ident)
            nc.vector.tensor_copy(
                out=s_grp[:, ps, :].bitcast(F32).rearrange("p (r u) -> p r u", u=2),
                in_=s_turned[:, 0 : 2 * P].rearrange("p (u r) -> p r u", u=2),
            )
        s_codes = keep.tile([P, 2, L], U32, name="s_codes", align_bytes=64)
        s_scales = keep.tile([P, 2, L], U8, name="s_scales", align_bytes=64)
        for ps in range(2):
            nc.vector.quantize_mx(out=s_codes[:, ps, :].bitcast(FP8X4), scales=s_scales[:, ps, :], in_=s_grp[:, ps, :])

        b1_banks = [spread(4 + half, "b1_bank%d" % half, half * F) for half in range(2)]
        b1_sb = keep.tile([P, 2, F], F32, name="b1_sb")
        for half in range(2):
            nc.scalar.copy(out=b1_sb[:, half, :], in_=b1_banks[half][:])
        g2_bank = spread(7, "g2_bank", D)
        neg_g2_sb = keep.tile([P, F], F32, name="neg_g2_sb")
        nc.scalar.activation(out=neg_g2_sb[:], in_=g2_bank[:], func=ACT.Copy, scale=-1.0)
        for turn in range(1, CLASSES):
            dst = perm[:, turn, :].rearrange("p (b a) -> p b a", a=CLASSES)
            src = ident.rearrange("p (b a) -> p b a", a=CLASSES)
            nc.scalar.copy(out=dst[:, :, 0 : CLASSES - turn], in_=src[:, :, turn:CLASSES])
            nc.scalar.copy(out=dst[:, :, CLASSES - turn : CLASSES], in_=src[:, :, 0:turn])
        nc.gpsimd.tensor_scalar(out=neg_g2[:], in0=g_cols[:, 1, :], scalar1=-1.0, scalar2=0.0, op0=ALU.mult, op1=ALU.add)

        h_banks = []
        for half in range(2):
            h_bank = bank(1 + half, "h_bank%d" % half)
            for ps in range(2):
                nc.tensor.matmul_mx(
                    out=h_bank[:],
                    lhsT=s_codes[:, ps, :].bitcast(FP8X4),
                    lhsT_scale=s_scales[:, ps, :],
                    rhs=w1_w[:, ps, half * 2 * F : (half + 1) * 2 * F].bitcast(FP4X4),
                    rhs_scale=w1_s[:, ps, half * F : (half + 1) * F],
                    start=(ps == 0),
                    stop=(ps == 1),
                )
            h_banks.append(h_bank)

        bo_bank = bank(0, "bo_bank")
        nc.tensor.matmul(out=bo_bank[:, 0:C], lhsT=ones[:], rhs=rows[:, D + F : D + F + C], start=True, stop=True)
        bo_sb = keep.tile([P, C], F32, name="bo_sb")
        nc.scalar.copy(out=bo_sb[:], in_=bo_bank[:, 0:C])

        q_tok = keep.tile([P, F], F32, name="q_tok")
        k_tok = keep.tile([P, F], F32, name="k_tok")
        qg2_tok = keep.tile([P, F], F32, name="qg2_tok")
        nkg2_tok = keep.tile([P, F], F32, name="nkg2_tok")
        for half, dst in enumerate((q_tok, k_tok)):
            nc.vector.tensor_tensor(
                out=dst[:].rearrange("i (t p) -> i t p", t=PACK),
                in0=h_banks[half][:].rearrange("i (p t) -> i t p", t=PACK),
                in1=b1_sb[:, half, :].rearrange("i (t p) -> i t p", t=PACK),
                op=ALU.add,
            )
        nc.vector.tensor_tensor(out=qg2_tok[:], in0=q_tok[:], in1=g2_bank[:], op=ALU.mult)
        nc.gpsimd.tensor_tensor(out=nkg2_tok[:], in0=k_tok[:], in1=neg_g2_sb[:], op=ALU.mult)
        parked = out[:, PARK : PARK + PACK, :].rearrange("i j c -> i (j c)")
        nc.sync.dma_start(out=parked, in_=qg2_tok[:])

        def turn_tokens(index, name, src):
            turned = bank(index, name)
            for t in range(PACK):
                dst = turned[:].rearrange("p (n t) -> p n t", t=PACK)[:, :, t]
                nc.tensor.transpose(dst, src[:, t * P : (t + 1) * P], ident)
            return turned

        q_bank = turn_tokens(3, "q_bank", q_tok)
        k_bank = turn_tokens(0, "k_bank", k_tok)
        qg2_bank = turn_tokens(4, "qg2_bank", qg2_tok)
        nkg2_bank = turn_tokens(5, "nkg2_bank", nkg2_tok)

        k_sb = keep.tile([P, F], F32, name="k_sb")
        k_planes = keep.tile([P, PACK, L], F32, name="k_planes")
        qg1 = keep.tile([P, SPAN, 2 * CLASSES * PACK], F32, name="qg1")
        qg2 = keep.tile([P, L, PACK], F32, name="qg2")
        nc.scalar.copy(out=k_sb[:], in_=k_bank[:])
        nc.scalar.copy(out=k_planes[:], in_=k_bank[:].rearrange("p (n t) -> p t n", t=PACK))
        nc.vector.tensor_tensor(
            out=qg1[:, :, 0:16].rearrange("p r (a t) -> p r a t", t=PACK),
            in0=q_bank[:].rearrange("p (a r t) -> p r a t", t=PACK, a=CLASSES),
            in1=g_cols[:, 0, :].unsqueeze(1).unsqueeze(1).to_broadcast([P, SPAN, CLASSES, PACK]),
            op=ALU.mult,
        )
        nc.scalar.copy(out=qg2[:].rearrange("p j t -> p (j t)"), in_=qg2_bank[:])

        q_rep = [keep.tile([P, run, F], F32, name="q_rep%d" % block) for block, run in enumerate(RUNS)]

        def load_replicas(block, lo, hi):
            for a in range(CLASSES):
                first = SPAN * a + STARTS[block]
                nc.sync.dma_start(
                    out=q_rep[block][a:P:CLASSES, lo:hi, :],
                    in_=parked[first + lo : first + hi, :].partition_broadcast(SPAN),
                )

        codes, results = {}, {}
        c_all = keep.tile([P, 24, F], BF16, name="c_all", align_bytes=64)
        diff_banks = [3, 4, 6, 7, 5]
        diff_count = [0]

        def fixed_on_scalar(grp, halves):
            count = len(halves)
            planes = work.tile([P, PACK, count * L], BF16, name="planes", tag="planes")
            for at, (kind, u) in enumerate(halves):
                j = grp["fixed"][u - grp["shifted"]]
                for t in range(PACK):
                    dst = planes[:, t, at * L : (at + 1) * L]
                    if kind == "diff":
                        nc.scalar.activation(
                            out=dst, in_=k_planes[:, t, :], func=ACT.Identity,
                            scale=neg_g2[:, t : t + 1], bias=qg2[:, j, t : t + 1],
                        )
                    else:
                        col = PACK * (j // SPAN) + t
                        nc.scalar.activation(
                            out=dst, in_=k_planes[:, t, :], func=ACT.Copy, scale=qg1[:, j % SPAN, col : col + 1]
                        )
            slot = grp["slot"][halves[0]]

            def interleave():
                nc.scalar.copy(
                    out=c_all[:, slot : slot + count, :].rearrange("p u (c i t) -> p (u c) t i", i=4, t=PACK),
                    in_=planes[:].rearrange("p t (c i) -> p c t i", i=4),
                )

            return interleave

        def shifted_diff(grp, u, dst):
            index = diff_banks[diff_count[0] % len(diff_banks)]
            diff_count[0] += 1
            diff_bank = bank(index, "diff_bank")
            for t in range(PACK):
                cols = slice(t * P, (t + 1) * P)
                nc.tensor.matmul(
                    out=diff_bank[:, cols], lhsT=nkg2_tok[:, cols], rhs=ident, is_transpose=True, start=True, stop=False
                )
                nc.tensor.matmul(
                    out=diff_bank[:, cols], lhsT=q_rep[grp["block"]][:, u, cols], rhs=perm[:, grp["turn"], :],
                    is_transpose=True, start=False, stop=True,
                )
            nc.scalar.copy(
                out=dst.rearrange("p (n t) -> p n t", t=PACK), in_=diff_bank[:].rearrange("p (t n) -> p n t", t=PACK)
            )

        def scalar_work(m):
            grp = groups[m]
            shifted = grp["shifted"]
            fixed = grp["on_scalar"][shifted:]
            steps = [fixed[at : at + 2] for at in range(0, len(fixed), 2)]
            ahead = min(2, shifted)
            steps = list(range(ahead)) + steps + list(range(ahead, shifted))
            pending = None
            for step in steps:
                following = None
                if isinstance(step, int):
                    shifted_diff(grp, step, c_all[:, grp["slot"][("diff", step)], :])
                else:
                    following = fixed_on_scalar(grp, step)
                if pending is not None:
                    pending()
                pending = following
            if pending is not None:
                pending()

        def products(engine, k_src, grp, first, count, row0, row1):
            lo, hi = 16 * row0, 16 * row1
            if first < grp["shifted"]:
                inner = 16
                tau = STARTS[grp["block"]] + first
                at = PACK * grp["turn"]
            else:
                inner = PACK
                j = grp["fixed"][first - grp["shifted"]]
                tau = j % SPAN
                at = PACK * (j // SPAN)
            shape = [P, count, (hi - lo) // inner, inner]
            slot = grp["slot"][("prod", first)]
            engine.tensor_tensor(
                out=c_all[:, slot : slot + count, lo:hi].rearrange("p u (b x) -> p u b x", x=inner),
                in0=k_src[:, lo:hi].rearrange("p (b x) -> p b x", x=inner).unsqueeze(1).to_broadcast(shape),
                in1=qg1[:, tau : tau + count, at : at + inner].unsqueeze(2).to_broadcast(shape),
                op=ALU.mult,
            )

        def evacuate(m, half):
            grp = groups[m]
            per_bank = grp["per_bank"]
            count = min(per_bank, grp["units"] - per_bank * half)
            if count <= 0:
                return
            acc, result = results[m]
            nc.vector.tensor_tensor(
                out=result[:, per_bank * half : per_bank * half + count, :],
                in0=acc[half][:, 0 : count * C].rearrange("p (u c) -> p u c", c=C),
                in1=bo_sb[:].unsqueeze(1).to_broadcast([P, count, C]),
                op=ALU.add,
            )

        def store(m):
            grp = groups[m]
            result = results[m][1]
            shifted = grp["shifted"]
            if shifted:
                for a in range(CLASSES):
                    j = SPAN * ((a + grp["turn"]) % CLASSES) + STARTS[grp["block"]]
                    nc.sync.dma_start(out=out[a:L:CLASSES, j : j + shifted, :], in_=result[a:P:CLASSES, 0:shifted, :])
            if grp["fixed"]:
                j = grp["fixed"][0]
                count = len(grp["fixed"])
                nc.sync.dma_start(out=out[:, j : j + count, :], in_=result[:, shifted : shifted + count, :])

        def vector_work(m):
            grp = groups[m]
            shared = len(grp["shared"])
            split = SPAN - grp["g_rows"]
            if grp["shifted"]:
                whole = shared - MIXED
                mixed = whole if m % 2 == 0 else 0
                products(nc.gpsimd, k_sb, grp, mixed, MIXED, split, SPAN)
                products(nc.vector, k_bank, grp, 0 if m % 2 == 0 else MIXED, whole, 0, SPAN)
                if split:
                    products(nc.vector, k_bank, grp, mixed, MIXED, 0, split)
            else:
                products(nc.gpsimd, k_sb, grp, 0, shared, split, SPAN)
                products(nc.vector, k_bank, grp, 0, shared, 0, split)
            if grp["shifted"] and grp["alone"]:
                products(nc.vector, k_bank, grp, shared, 1, 0, SPAN)
            if grp["v_diffs"]:
                count = grp["v_diffs"]
                j = grp["fixed"][grp["units"] - count]
                slot = grp["slot"][("diff", grp["units"] - count)]
                shape = [P, count, L, PACK]
                nc.vector.tensor_tensor(
                    out=c_all[:, slot : slot + count, :].rearrange("p u (n t) -> p u n t", t=PACK),
                    in0=nkg2_bank[:].rearrange("p (n t) -> p n t", t=PACK).unsqueeze(1).to_broadcast(shape),
                    in1=qg2[:, j : j + count, :].unsqueeze(2).to_broadcast(shape),
                    op=ALU.add,
                )
            if m:
                evacuate(m - 1, 0)
                evacuate(m - 1, 1)
                store(m - 1)

        def quantise(m):
            grp = groups[m]
            count, first = len(grp["halves"]), grp["first"]
            words = work.tile([P, 16 * L], U32, name="words", tag="words", align_bytes=64)
            scales = work.tile([P, 16 * L], U8, name="scales", tag="scales", align_bytes=64)
            for start, width in power_of_two_runs(count):
                at = start if m % 2 == 0 else count - start - width
                cols = slice(at * L, (at + width) * L)
                nc.vector.quantize_mx(
                    out=words[:, cols].bitcast(FP8X4),
                    scales=scales[:, cols],
                    in_=c_all[:, first + at : first + at + width, :].rearrange("p u x -> p (u x)"),
                )
            codes[m] = {
                half: (words[:, at * L : (at + 1) * L], scales[:, at * L : (at + 1) * L])
                for at, half in enumerate(grp["halves"])
            }

        def multiply(m):
            grp = groups[m]
            per_bank = grp["per_bank"]
            acc = [bank(1 + half, "acc%d" % half) for half in range(-(-grp["units"] // per_bank))]
            for u in range(grp["units"]):
                for ps, kind in enumerate(("prod", "diff")):
                    words, scales = codes[m][(kind, u)]
                    nc.tensor.matmul_mx(
                        out=acc[u // per_bank][:, (u % per_bank) * C : (u % per_bank + 1) * C],
                        lhsT=words.bitcast(FP8X4),
                        lhsT_scale=scales,
                        rhs=wo_w[:, ps, :].bitcast(FP4X4),
                        rhs_scale=wo_s[:, ps, :],
                        start=(ps == 0),
                        stop=(ps == 1),
                    )
            result = work.tile([P, 8, C], F32, name="result", tag="result", bufs=3)
            results[m] = (acc, result)

        load_replicas(0, 0, 3)
        load_replicas(0, 3, RUNS[0])
        scalar_work(0)
        for m in range(len(groups)):
            vector_work(m)
            if m + 1 < len(RUNS):
                load_replicas(m + 1, 0, RUNS[m + 1])
            if m + 1 < len(groups):
                scalar_work(m + 1)
            if m == 0:
                nc.vector.tensor_copy(out=qg1[:, :, 16:28], in_=qg1[:, :, 0:12])
            quantise(m)
            multiply(m)
        last = len(groups) - 1
        for half in range(2):
            evacuate(last, half)
            j = groups[last]["fixed"][2 * half]
            nc.sync.dma_start(out=out[:, j : j + 2, :], in_=results[last][1][:, 2 * half : 2 * half + 2, :])
